import numpy as np
import ml_dtypes


def mxq(x, axis, fmt="e4m3"):
    dtype, down = {"e4m3": (ml_dtypes.float8_e4m3fn, 7), "e5m2": (ml_dtypes.float8_e5m2, 14)}[fmt]
    v = np.moveaxis(np.asarray(x, np.float32).astype(ml_dtypes.bfloat16).astype(np.float64), axis, -1)
    blocks = v.reshape(v.shape[:-1] + (-1, 32))
    amax = np.abs(blocks).max(-1, keepdims=True)
    byte = np.maximum(np.where(amax > 0, np.frexp(amax)[1] - 1 + 127, 0) - down, 1)
    scale = np.exp2(byte - 127.0)
    codes = (blocks / scale).astype(np.float32).astype(dtype).astype(np.float64)
    return np.moveaxis((codes * scale).reshape(v.shape), -1, axis)


WIDE = False


def mx_kscale(k):
    if not WIDE:
        return np.ones(k)
    levels = np.array([10, -10, 5, -5, 0])
    if k % 512:
        return np.exp2(np.random.permutation(np.resize(levels, k // 32))).repeat(32)
    a = np.empty((k // 512, 16))
    for p in range(k // 512):
        a[p, :8] = np.random.permutation(np.resize(levels, 8))
        for g in range(8):
            far = levels[np.abs(levels - a[p, g]) >= 10]
            a[p, g + 8] = far[np.random.randint(len(far))]
    return np.exp2(a.ravel()).repeat(32)


def f64(x):
    return np.asarray(x).astype(np.float64)


def striped(idx):
    return np.tile(np.asarray(idx).reshape(-1, 16).T, (8, 1)).astype(np.uint16)


def unstriped(offs):
    return offs[:16].T.reshape(-1).astype(np.int64)


E2M1 = np.array([0.0, 0.5, 1.0, 1.5, 2.0, 3.0, 4.0, 6.0, -0.0, -0.5, -1.0, -1.5, -2.0, -3.0, -4.0, -6.0])


def pack_weight(w, fmt):
    k, n = w.shape
    w = f64(np.asarray(w, np.float32).astype(ml_dtypes.bfloat16)).reshape(k // 32, 32, n)
    amax = np.abs(w).max(1)
    if fmt == "e4m3":
        byte = np.frexp(amax)[1] - 1 + 127 - 7
    else:
        mant, ex = np.frexp(amax / 6.0)
        byte = np.where(mant > 0.5, ex, ex - 1) + 127
    byte = np.clip(np.where(amax > 0, byte, 1), 1, 254)
    scaled = (w * np.exp2(127.0 - byte)[:, None, :]).reshape(k, n).astype(np.float32)
    by_word = np.ascontiguousarray(scaled.reshape(k // 512, 128, 4, n).transpose(0, 1, 3, 2))
    if fmt == "e4m3":
        words = by_word.astype(ml_dtypes.float8_e4m3fn).view(np.uint8)
    else:
        c = by_word.astype(ml_dtypes.float4_e2m1fn).view(np.uint8) & 0xF
        words = (c[..., 0::2] | (c[..., 1::2] << 4)).reshape(k // 512, 128, 2 * n)
    return np.ascontiguousarray(words), np.ascontiguousarray(byte.astype(np.uint8).reshape(k // 512, 16, n))


def unpack_weight(words, scales, fmt):
    g, _, n = scales.shape
    words = np.ascontiguousarray(words).reshape(g, 128, n, -1)
    if fmt == "e4m3":
        vals = words.view(ml_dtypes.float8_e4m3fn).astype(np.float64)
    else:
        nib = np.empty((g, 128, n, 4), np.uint8)
        nib[..., 0::2] = words & 0xF
        nib[..., 1::2] = words >> 4
        vals = E2M1[nib]
    vals = vals * np.repeat(np.exp2(scales.astype(np.float64) - 127.0), 8, axis=1)[..., None]
    return vals.transpose(0, 1, 3, 2).reshape(g * 512, n)


D, T, I, J, U, Z, E, N = 512, 2048, 512, 512, 1024, 1024, 512, 64


def setup_inputs():
    n = np.random.standard_normal
    idx = np.random.permutation(T)[:I]
    idx2 = np.random.permutation(U)[:J]
    idx3 = np.random.permutation(Z)[:J]
    fd = mx_kscale(D)
    fi = mx_kscale(I)
    ti = np.ones(T)
    ti[idx] = fi
    keysp = pack_weight(n((D, T)) / fd[:, None], "e4m3")
    return {
        "keys_words": keysp[0],
        "keys_scales": keysp[1],
        "notes": (n((D, U)) * 1.0 / np.sqrt(D) * fd[:, None]).astype(np.float32),
        "given": (np.random.uniform(0.3, 1.7, (I, Z))).astype(np.float32),
        "rowf": (np.random.uniform(0.02, 0.08, (I, 1)) * fi[:, None]).astype(np.float32),
        "vals": (n((E, T)) / ti).astype(np.float32),
        "offs": striped(idx),
        "offs2": striped(idx2),
        "offs3": striped(idx3),
    }


def reference(keys_words, keys_scales, notes, given, rowf, vals, offs, offs2, offs3):
    idx = unstriped(offs)
    idx2 = unstriped(offs2)
    idx3 = unstriped(offs3)
    keysu = unpack_weight(keys_words, keys_scales, "e4m3")
    keysidxg = keysu[:, idx]
    notesidx2q = mxq(f64(notes)[:, idx2], 0, "e4m3")
    g1 = keysidxg.T @ notesidx2q
    g0 = g1 * f64(given)[:, idx3]
    gr1 = g0 * f64(rowf)
    vt1 = f64(vals)[:, idx].T
    vt1q = mxq(vt1, 0, "e4m3")
    gr1q = mxq(gr1, 0, "e4m3")
    o = vt1q.T @ gr1q
    y = o.reshape(E, N, J // N).max(axis=2)
    return y

@@ -1,0 +1,203 @@
+from contextlib import ExitStack
+
+import concourse.mybir as mybir
+from concourse.masks import make_identity
+
+F32 = mybir.dt.float32
+BF16 = mybir.dt.bfloat16
+I32 = mybir.dt.int32
+U32 = mybir.dt.uint32
+U16 = mybir.dt.uint16
+U8 = mybir.dt.uint8
+FP8X4 = mybir.dt.float8_e4m3fn_x4
+COPY = mybir.ActivationFunctionType.Copy
+MULT = mybir.AluOpType.mult
+MAX = mybir.AluOpType.max
+AXIS_X = mybir.AxisListType.X
+
+P = 128
+PACK = 4
+LISTED = 512
+TOKENS = 2048
+STORE = 1024
+RUN = 8
+HALF = LISTED // 2
+WEAVE_SPLIT = 336
+FLOPS = 2 * 2 * 512 * 512 * 512
+
+
+def tile_attend_tab_timestable_bestruns_kernel(
+    tc, keys_words, keys_scales, notes, given, rowf, vals, offs, offs2, offs3, out
+):
+    nc = tc.nc
+    with ExitStack() as ctx:
+        lists = ctx.enter_context(tc.tile_pool(name="lists", bufs=1))
+        pool = ctx.enter_context(tc.tile_pool(name="pool", bufs=1))
+        ring = ctx.enter_context(tc.tile_pool(name="ring", bufs=2))
+        acc = ctx.enter_context(tc.psum_pool(name="acc", bufs=6))
+        turn = ctx.enter_context(tc.psum_pool(name="turn", bufs=2))
+
+        tok_list = lists.tile([P, LISTED // 16], U16, name="tok_list")
+        note_list = lists.tile([P, LISTED // 16], U16, name="note_list")
+        col_list = lists.tile([P, LISTED // 16], U16, name="col_list")
+
+        notes_v = notes.rearrange("(p t) u -> p t u", t=PACK)
+        given_v = given.rearrange("(p t) z -> p t z", t=PACK)
+        vals_v = vals.rearrange("(p c) x -> p c x", c=PACK)
+        out_v = out.rearrange("(p c) n -> p c n", c=PACK)
+
+        key_bytes = pool.tile([P, TOKENS], U8, name="key_bytes")
+        row_factor = pool.tile([P, PACK], F32, name="row_factor")
+        nc.vector.memset(key_bytes[:].bitcast(I32), 0)
+        ident = pool.tile([P, P], F32, name="ident")
+        make_identity(nc, ident[:])
+
+        def load_planes(source, first, last, name):
+            tile = pool.tile([P, last - first, STORE], F32, name=name)
+            nc.sync.dma_start(out=tile[:], in_=source[:, first:last, :])
+            return [tile[:, t, :] for t in range(last - first)]
+
+        key_words = pool.tile([P, TOKENS], I32, name="key_words")
+        nc.sync.dma_start(out=note_list[:], in_=offs2)
+        note_store = load_planes(notes_v, 0, 1, "note_store0")
+        nc.sync.dma_start(out=tok_list[:], in_=offs)
+        nc.sync.dma_start(out=key_words[:], in_=keys_words[0].rearrange("p c r -> p (c r)").bitcast(I32))
+        for q in range(4):
+            nc.sync.dma_start(
+                out=key_bytes[32 * q : 32 * q + 4, :].bitcast(I32),
+                in_=keys_scales[0, 4 * q : 4 * q + 4, :].bitcast(I32),
+            )
+        note_store = note_store + load_planes(notes_v, 1, 2, "note_store1")
+        note_store = note_store + load_planes(notes_v, 2, 4, "note_store23")
+        nc.sync.dma_start(out=col_list[:], in_=offs3)
+        given_wide = load_planes(given_v, 0, 2, "given_wide01")
+        nc.sync.dma_start(out=row_factor[:], in_=rowf.rearrange("(p t) o -> p (t o)", t=PACK))
+        given_wide = given_wide + load_planes(given_v, 2, 3, "given_wide2")
+        given_wide = given_wide + load_planes(given_v, 3, 4, "given_wide3")
+        val_pools = [pool.tile([P, TOKENS], F32, name=f"val_pool{c}", align_bytes=64) for c in range(PACK)]
+        for c in range(PACK):
+            nc.sync.dma_start(out=val_pools[c][:], in_=vals_v[:, c, :])
+
+        def gather(engine, dst, window, offsets):
+            if engine == "vector":
+                nc.vector.tensor_copy(out=dst, in_=window.indirect(offsets))
+            else:
+                nc.scalar.activation(out=dst, in_=window.indirect(offsets), func=COPY)
+
+        def gather_shared(dst, window, offsets):
+            gather("vector", dst[:, :HALF], window, offsets[:, : HALF // 16])
+            gather("scalar", dst[:, HALF:], window, offsets[:, HALF // 16 :])
+
+        def weave(copy, dst, src, first, last):
+            copy(
+                out=dst[:, first * PACK : last * PACK].rearrange("p (c i t) -> p c t i", i=4, t=PACK),
+                in_=src[:, :, first:last].rearrange("p t (c i) -> p c t i", i=4),
+            )
+
+        key_codes = pool.tile([P, PACK, P], U32, name="key_codes", align_bytes=64)
+        key_scales = pool.tile([P, PACK, P], U8, name="key_scales", align_bytes=64)
+        nc.vector.tensor_copy(
+            out=key_codes[:].rearrange("p t m -> p m t"), in_=key_words[:].bitcast(U32).indirect(tok_list[:])
+        )
+
+        note_planes = pool.tile([P, PACK, LISTED], F32, name="note_planes")
+        nc.vector.tensor_copy(
+            out=key_scales[:].rearrange("p t m -> p m t"), in_=key_bytes[:].indirect(tok_list[:])
+        )
+        for t in range(PACK):
+            gather("vector" if t == 2 else "scalar", note_planes[:, t, :], note_store[t], note_list[:])
+        note_woven = pool.tile([P, LISTED * PACK], BF16, name="note_woven", align_bytes=64)
+        weave(nc.vector.tensor_copy, note_woven, note_planes, 0, WEAVE_SPLIT)
+        weave(nc.scalar.copy, note_woven, note_planes, WEAVE_SPLIT, LISTED)
+        note_codes = pool.tile([P, LISTED], U32, name="note_codes", align_bytes=64)
+        note_scales = pool.tile([P, LISTED], U8, name="note_scales", align_bytes=64)
+        nc.vector.quantize_mx(out=note_codes[:].bitcast(FP8X4), scales=note_scales[:], in_=note_woven[:])
+
+        given_planes = pool.tile([P, PACK, LISTED], F32, name="given_planes")
+        table_planes = pool.tile([P, PACK, LISTED], BF16, name="table_planes")
+        for t in range(PACK):
+            gather("vector" if t == 1 else "scalar", given_planes[:, t, :], given_wide[t], col_list[:])
+        for t in range(PACK):
+            scores = acc.tile([P, LISTED], F32, name="bank")
+            nc.tensor.matmul_mx(
+                out=scores[:],
+                lhsT=key_codes[:, t, :].bitcast(FP8X4),
+                lhsT_scale=key_scales[:, t, :],
+                rhs=note_codes[:].bitcast(FP8X4),
+                rhs_scale=note_scales[:],
+                start=True,
+                stop=True,
+            )
+            nc.vector.scalar_tensor_tensor(
+                out=table_planes[:, t, :],
+                in0=scores[:],
+                scalar=row_factor[:, t : t + 1],
+                in1=given_planes[:, t, :],
+                op0=MULT,
+                op1=MULT,
+            )
+        table_woven = pool.tile([P, LISTED * PACK], BF16, name="table_woven", align_bytes=64)
+        weave(nc.vector.tensor_copy, table_woven, table_planes, 0, WEAVE_SPLIT)
+        weave(nc.scalar.copy, table_woven, table_planes, WEAVE_SPLIT, LISTED)
+        table_codes = pool.tile([P, LISTED], U32, name="table_codes", align_bytes=64)
+        table_scales = pool.tile([P, LISTED], U8, name="table_scales", align_bytes=64)
+        nc.vector.quantize_mx(out=table_codes[:].bitcast(FP8X4), scales=table_scales[:], in_=table_woven[:])
+
+        def turn_values(c):
+            picked = ring.tile([P, LISTED], BF16, name="picked")
+            if c == 0:
+                gather("scalar", picked[:], val_pools[c][:], tok_list[:])
+            else:
+                gather_shared(picked, val_pools[c][:], tok_list)
+            pairs = picked[:].bitcast(F32)
+            turned = turn.tile([P, 2, P], F32, name="turned")
+            for u in range(2):
+                nc.tensor.transpose(turned[:, u, :], pairs[:, u : HALF : 2], ident[:])
+            return turned
+
+        def quantize_values(c, turned):
+            woven = pool.tile([P, P * PACK], BF16, name="val_woven", tag=f"val_pool{c + 1}", align_bytes=64)
+            nc.scalar.copy(
+                out=woven[:].bitcast(F32).rearrange("p (e u) -> p e u", u=2),
+                in_=turned[:].rearrange("p u e -> p e u"),
+            )
+            codes = ring.tile([P, P], U32, name="val_codes", align_bytes=64, bufs=4)
+            scales = ring.tile([P, P], U8, name="val_scales", align_bytes=64, bufs=4)
+            nc.vector.quantize_mx(out=codes[:].bitcast(FP8X4), scales=scales[:], in_=woven[:])
+            return codes, scales
+
+        def best_runs(operand, best):
+            codes, scales = operand
+            for h in range(2):
+                cols = slice(h * HALF, (h + 1) * HALF)
+                sums = acc.tile([P, HALF], F32, name="bank")
+                nc.tensor.matmul_mx(
+                    out=sums[:],
+                    lhsT=codes[:].bitcast(FP8X4),
+                    lhsT_scale=scales[:],
+                    rhs=table_codes[:, cols].bitcast(FP8X4),
+                    rhs_scale=table_scales[:, cols],
+                    start=True,
+                    stop=True,
+                )
+                nc.vector.tensor_reduce(
+                    out=best[:, h * (HALF // RUN) : (h + 1) * (HALF // RUN)],
+                    in_=sums[:].rearrange("p (n k) -> p n k", k=RUN),
+                    axis=AXIS_X,
+                    op=MAX,
+                )
+
+        turned = [turn_values(0)]
+        operands = []
+        for c in range(PACK):
+            if c + 1 < PACK:
+                turned.append(turn_values(c + 1))
+            operands.append(quantize_values(c, turned[c]))
+            if c in (1, 2):
+                best = pool.tile([P, LISTED // RUN], F32, name="best", tag=f"val_pool{c + 1}", align_bytes=64)
+                best_runs(operands[c - 1], best)
+                nc.sync.dma_start(out=out_v[:, c - 1, :], in_=best[:])
+        best_late = pool.tile([P, 2, LISTED // RUN], F32, name="best_late", tag="val_pool4", align_bytes=64)
+        best_runs(operands[2], best_late[:, 0, :])
+        best_runs(operands[3], best_late[:, 1, :])
+        nc.sync.dma_start(out=out_v[:, 2:4, :], in_=best_late[:])

@@ -52,16 +52,16 @@ def tile_attend_tab_timestable_bestruns_kernel(
         ident = pool.tile([P, P], F32, name="ident")
         make_identity(nc, ident[:])
 
-        def load_planes(source, first, last, name):
+        def load_planes(source, first, last, name, queue=nc.sync):
             tile = pool.tile([P, last - first, STORE], F32, name=name)
-            nc.sync.dma_start(out=tile[:], in_=source[:, first:last, :])
+            queue.dma_start(out=tile[:], in_=source[:, first:last, :])
             return [tile[:, t, :] for t in range(last - first)]
 
         key_words = pool.tile([P, TOKENS], I32, name="key_words")
+        note_store = load_planes(notes_v, 0, 1, "note_store0", nc.scalar)
         nc.sync.dma_start(out=note_list[:], in_=offs2)
-        note_store = load_planes(notes_v, 0, 1, "note_store0")
         nc.sync.dma_start(out=tok_list[:], in_=offs)
-        nc.sync.dma_start(out=key_words[:], in_=keys_words[0].rearrange("p c r -> p (c r)").bitcast(I32))
+        nc.scalar.dma_start(out=key_words[:], in_=keys_words[0].rearrange("p c r -> p (c r)").bitcast(I32))
         for q in range(4):
             nc.sync.dma_start(
                 out=key_bytes[32 * q : 32 * q + 4, :].bitcast(I32),

@@ -67,11 +67,11 @@ def tile_attend_tab_timestable_bestruns_kernel(
                 out=key_bytes[32 * q : 32 * q + 4, :].bitcast(I32),
                 in_=keys_scales[0, 4 * q : 4 * q + 4, :].bitcast(I32),
             )
+        nc.scalar.dma_start(out=row_factor[:], in_=rowf.rearrange("(p t) o -> p (t o)", t=PACK))
         note_store = note_store + load_planes(notes_v, 1, 2, "note_store1")
         note_store = note_store + load_planes(notes_v, 2, 4, "note_store23")
         nc.sync.dma_start(out=col_list[:], in_=offs3)
         given_wide = load_planes(given_v, 0, 2, "given_wide01")
-        nc.sync.dma_start(out=row_factor[:], in_=rowf.rearrange("(p t) o -> p (t o)", t=PACK))
         given_wide = given_wide + load_planes(given_v, 2, 3, "given_wide2")
         given_wide = given_wide + load_planes(given_v, 3, 4, "given_wide3")
         val_pools = [pool.tile([P, TOKENS], F32, name=f"val_pool{c}", align_bytes=64) for c in range(PACK)]
@@ -137,15 +137,14 @@ def tile_attend_tab_timestable_bestruns_kernel(
                 op1=MULT,
             )
         table_woven = pool.tile([P, LISTED * PACK], BF16, name="table_woven", align_bytes=64)
-        weave(nc.vector.tensor_copy, table_woven, table_planes, 0, WEAVE_SPLIT)
-        weave(nc.scalar.copy, table_woven, table_planes, WEAVE_SPLIT, LISTED)
+        weave(nc.vector.tensor_copy, table_woven, table_planes, 0, LISTED)
         table_codes = pool.tile([P, LISTED], U32, name="table_codes", align_bytes=64)
         table_scales = pool.tile([P, LISTED], U8, name="table_scales", align_bytes=64)
         nc.vector.quantize_mx(out=table_codes[:].bitcast(FP8X4), scales=table_scales[:], in_=table_woven[:])
 
         def turn_values(c):
             picked = ring.tile([P, LISTED], BF16, name="picked")
-            if c == 0:
+            if c < 2:
                 gather("scalar", picked[:], val_pools[c][:], tok_list[:])
             else:
                 gather_shared(picked, val_pools[c][:], tok_list)
@@ -198,6 +197,6 @@ def tile_attend_tab_timestable_bestruns_kernel(
                 best_runs(operands[c - 1], best)
                 nc.sync.dma_start(out=out_v[:, c - 1, :], in_=best[:])
         best_late = pool.tile([P, 2, LISTED // RUN], F32, name="best_late", tag="val_pool4", align_bytes=64)
-        best_runs(operands[2], best_late[:, 0, :])
-        best_runs(operands[3], best_late[:, 1, :])
-        nc.sync.dma_start(out=out_v[:, 2:4, :], in_=best_late[:])
+        for c in (2, 3):
+            best_runs(operands[c], best_late[:, c - 2, :])
+            nc.sync.dma_start(out=out_v[:, c, :], in_=best_late[:, c - 2, :])

from contextlib import ExitStack

import concourse.mybir as mybir
from concourse.masks import make_identity

F32 = mybir.dt.float32
BF16 = mybir.dt.bfloat16
I32 = mybir.dt.int32
U32 = mybir.dt.uint32
U16 = mybir.dt.uint16
U8 = mybir.dt.uint8
FP8X4 = mybir.dt.float8_e4m3fn_x4
COPY = mybir.ActivationFunctionType.Copy
MULT = mybir.AluOpType.mult
MAX = mybir.AluOpType.max
AXIS_X = mybir.AxisListType.X

P = 128
PACK = 4
LISTED = 512
TOKENS = 2048
STORE = 1024
RUN = 8
HALF = LISTED // 2
WEAVE_SPLIT = 336
FLOPS = 2 * 2 * 512 * 512 * 512


def tile_attend_tab_timestable_bestruns_kernel(
    tc, keys_words, keys_scales, notes, given, rowf, vals, offs, offs2, offs3, out
):
    nc = tc.nc
    with ExitStack() as ctx:
        lists = ctx.enter_context(tc.tile_pool(name="lists", bufs=1))
        pool = ctx.enter_context(tc.tile_pool(name="pool", bufs=1))
        ring = ctx.enter_context(tc.tile_pool(name="ring", bufs=2))
        acc = ctx.enter_context(tc.psum_pool(name="acc", bufs=6))
        turn = ctx.enter_context(tc.psum_pool(name="turn", bufs=2))

        tok_list = lists.tile([P, LISTED // 16], U16, name="tok_list")
        note_list = lists.tile([P, LISTED // 16], U16, name="note_list")
        col_list = lists.tile([P, LISTED // 16], U16, name="col_list")

        notes_v = notes.rearrange("(p t) u -> p t u", t=PACK)
        given_v = given.rearrange("(p t) z -> p t z", t=PACK)
        vals_v = vals.rearrange("(p c) x -> p c x", c=PACK)
        out_v = out.rearrange("(p c) n -> p c n", c=PACK)

        key_bytes = pool.tile([P, TOKENS], U8, name="key_bytes")
        row_factor = pool.tile([P, PACK], F32, name="row_factor")
        nc.vector.memset(key_bytes[:].bitcast(I32), 0)
        ident = pool.tile([P, P], F32, name="ident")
        make_identity(nc, ident[:])

        def load_planes(source, first, last, name, queue=nc.sync):
            tile = pool.tile([P, last - first, STORE], F32, name=name)
            queue.dma_start(out=tile[:], in_=source[:, first:last, :])
            return [tile[:, t, :] for t in range(last - first)]

        key_words = pool.tile([P, TOKENS], I32, name="key_words")
        note_store = load_planes(notes_v, 0, 1, "note_store0", nc.scalar)
        nc.sync.dma_start(out=note_list[:], in_=offs2)
        nc.sync.dma_start(out=tok_list[:], in_=offs)
        nc.scalar.dma_start(out=key_words[:], in_=keys_words[0].rearrange("p c r -> p (c r)").bitcast(I32))
        for q in range(4):
            nc.sync.dma_start(
                out=key_bytes[32 * q : 32 * q + 4, :].bitcast(I32),
                in_=keys_scales[0, 4 * q : 4 * q + 4, :].bitcast(I32),
            )
        nc.scalar.dma_start(out=row_factor[:], in_=rowf.rearrange("(p t) o -> p (t o)", t=PACK))
        note_store = note_store + load_planes(notes_v, 1, 2, "note_store1")
        note_store = note_store + load_planes(notes_v, 2, 4, "note_store23")
        nc.sync.dma_start(out=col_list[:], in_=offs3)
        given_wide = load_planes(given_v, 0, 2, "given_wide01")
        given_wide = given_wide + load_planes(given_v, 2, 3, "given_wide2")
        given_wide = given_wide + load_planes(given_v, 3, 4, "given_wide3")
        val_pools = [pool.tile([P, TOKENS], F32, name=f"val_pool{c}", align_bytes=64) for c in range(PACK)]
        for c in range(PACK):
            nc.sync.dma_start(out=val_pools[c][:], in_=vals_v[:, c, :])

        def gather(engine, dst, window, offsets):
            if engine == "vector":
                nc.vector.tensor_copy(out=dst, in_=window.indirect(offsets))
            else:
                nc.scalar.activation(out=dst, in_=window.indirect(offsets), func=COPY)

        def gather_shared(dst, window, offsets):
            gather("vector", dst[:, :HALF], window, offsets[:, : HALF // 16])
            gather("scalar", dst[:, HALF:], window, offsets[:, HALF // 16 :])

        def weave(copy, dst, src, first, last):
            copy(
                out=dst[:, first * PACK : last * PACK].rearrange("p (c i t) -> p c t i", i=4, t=PACK),
                in_=src[:, :, first:last].rearrange("p t (c i) -> p c t i", i=4),
            )

        key_codes = pool.tile([P, PACK, P], U32, name="key_codes", align_bytes=64)
        key_scales = pool.tile([P, PACK, P], U8, name="key_scales", align_bytes=64)
        nc.vector.tensor_copy(
            out=key_codes[:].rearrange("p t m -> p m t"), in_=key_words[:].bitcast(U32).indirect(tok_list[:])
        )

        note_planes = pool.tile([P, PACK, LISTED], F32, name="note_planes")
        nc.vector.tensor_copy(
            out=key_scales[:].rearrange("p t m -> p m t"), in_=key_bytes[:].indirect(tok_list[:])
        )
        for t in range(PACK):
            gather("vector" if t == 2 else "scalar", note_planes[:, t, :], note_store[t], note_list[:])
        note_woven = pool.tile([P, LISTED * PACK], BF16, name="note_woven", align_bytes=64)
        weave(nc.vector.tensor_copy, note_woven, note_planes, 0, WEAVE_SPLIT)
        weave(nc.scalar.copy, note_woven, note_planes, WEAVE_SPLIT, LISTED)
        note_codes = pool.tile([P, LISTED], U32, name="note_codes", align_bytes=64)
        note_scales = pool.tile([P, LISTED], U8, name="note_scales", align_bytes=64)
        nc.vector.quantize_mx(out=note_codes[:].bitcast(FP8X4), scales=note_scales[:], in_=note_woven[:])

        given_planes = pool.tile([P, PACK, LISTED], F32, name="given_planes")
        table_planes = pool.tile([P, PACK, LISTED], BF16, name="table_planes")
        for t in range(PACK):
            gather("vector" if t == 1 else "scalar", given_planes[:, t, :], given_wide[t], col_list[:])
        for t in range(PACK):
            scores = acc.tile([P, LISTED], F32, name="bank")
            nc.tensor.matmul_mx(
                out=scores[:],
                lhsT=key_codes[:, t, :].bitcast(FP8X4),
                lhsT_scale=key_scales[:, t, :],
                rhs=note_codes[:].bitcast(FP8X4),
                rhs_scale=note_scales[:],
                start=True,
                stop=True,
            )
            nc.vector.scalar_tensor_tensor(
                out=table_planes[:, t, :],
                in0=scores[:],
                scalar=row_factor[:, t : t + 1],
                in1=given_planes[:, t, :],
                op0=MULT,
                op1=MULT,
            )
        table_woven = pool.tile([P, LISTED * PACK], BF16, name="table_woven", align_bytes=64)
        weave(nc.vector.tensor_copy, table_woven, table_planes, 0, LISTED)
        table_codes = pool.tile([P, LISTED], U32, name="table_codes", align_bytes=64)
        table_scales = pool.tile([P, LISTED], U8, name="table_scales", align_bytes=64)
        nc.vector.quantize_mx(out=table_codes[:].bitcast(FP8X4), scales=table_scales[:], in_=table_woven[:])

        def turn_values(c):
            picked = ring.tile([P, LISTED], BF16, name="picked")
            if c < 2:
                gather("scalar", picked[:], val_pools[c][:], tok_list[:])
            else:
                gather_shared(picked, val_pools[c][:], tok_list)
            pairs = picked[:].bitcast(F32)
            turned = turn.tile([P, 2, P], F32, name="turned")
            for u in range(2):
                nc.tensor.transpose(turned[:, u, :], pairs[:, u : HALF : 2], ident[:])
            return turned

        def quantize_values(c, turned):
            woven = pool.tile([P, P * PACK], BF16, name="val_woven", tag=f"val_pool{c + 1}", align_bytes=64)
            nc.scalar.copy(
                out=woven[:].bitcast(F32).rearrange("p (e u) -> p e u", u=2),
                in_=turned[:].rearrange("p u e -> p e u"),
            )
            codes = ring.tile([P, P], U32, name="val_codes", align_bytes=64, bufs=4)
            scales = ring.tile([P, P], U8, name="val_scales", align_bytes=64, bufs=4)
            nc.vector.quantize_mx(out=codes[:].bitcast(FP8X4), scales=scales[:], in_=woven[:])
            return codes, scales

        def best_runs(operand, best):
            codes, scales = operand
            for h in range(2):
                cols = slice(h * HALF, (h + 1) * HALF)
                sums = acc.tile([P, HALF], F32, name="bank")
                nc.tensor.matmul_mx(
                    out=sums[:],
                    lhsT=codes[:].bitcast(FP8X4),
                    lhsT_scale=scales[:],
                    rhs=table_codes[:, cols].bitcast(FP8X4),
                    rhs_scale=table_scales[:, cols],
                    start=True,
                    stop=True,
                )
                nc.vector.tensor_reduce(
                    out=best[:, h * (HALF // RUN) : (h + 1) * (HALF // RUN)],
                    in_=sums[:].rearrange("p (n k) -> p n k", k=RUN),
                    axis=AXIS_X,
                    op=MAX,
                )

        turned = [turn_values(0)]
        operands = []
        for c in range(PACK):
            if c + 1 < PACK:
                turned.append(turn_values(c + 1))
            operands.append(quantize_values(c, turned[c]))
            if c in (1, 2):
                best = pool.tile([P, LISTED // RUN], F32, name="best", tag=f"val_pool{c + 1}", align_bytes=64)
                best_runs(operands[c - 1], best)
                nc.sync.dma_start(out=out_v[:, c - 1, :], in_=best[:])
        best_late = pool.tile([P, 2, LISTED // RUN], F32, name="best_late", tag="val_pool4", align_bytes=64)
        for c in (2, 3):
            best_runs(operands[c], best_late[:, c - 2, :])
            nc.sync.dma_start(out=out_v[:, c, :], in_=best_late[:, c - 2, :])
